import numpy as np
import ml_dtypes


def mxq(x, axis, fmt="e4m3"):
    dtype, down = {"e4m3": (ml_dtypes.float8_e4m3fn, 7), "e5m2": (ml_dtypes.float8_e5m2, 14)}[fmt]
    v = np.moveaxis(np.asarray(x, np.float32).astype(ml_dtypes.bfloat16).astype(np.float64), axis, -1)
    blocks = v.reshape(v.shape[:-1] + (-1, 32))
    amax = np.abs(blocks).max(-1, keepdims=True)
    byte = np.maximum(np.where(amax > 0, np.frexp(amax)[1] - 1 + 127, 0) - down, 1)
    scale = np.exp2(byte - 127.0)
    codes = (blocks / scale).astype(np.float32).astype(dtype).astype(np.float64)
    return np.moveaxis((codes * scale).reshape(v.shape), -1, axis)


WIDE = False


def mx_kscale(k):
    if not WIDE:
        return np.ones(k)
    levels = np.array([10, -10, 5, -5, 0])
    if k % 512:
        return np.exp2(np.random.permutation(np.resize(levels, k // 32))).repeat(32)
    a = np.empty((k // 512, 16))
    for p in range(k // 512):
        a[p, :8] = np.random.permutation(np.resize(levels, 8))
        for g in range(8):
            far = levels[np.abs(levels - a[p, g]) >= 10]
            a[p, g + 8] = far[np.random.randint(len(far))]
    return np.exp2(a.ravel()).repeat(32)


def f64(x):
    return np.asarray(x).astype(np.float64)


def striped(idx):
    return np.tile(np.asarray(idx).reshape(-1, 16).T, (8, 1)).astype(np.uint16)


def unstriped(offs):
    return offs[:16].T.reshape(-1).astype(np.int64)


E2M1 = np.array([0.0, 0.5, 1.0, 1.5, 2.0, 3.0, 4.0, 6.0, -0.0, -0.5, -1.0, -1.5, -2.0, -3.0, -4.0, -6.0])


def pack_weight(w, fmt):
    k, n = w.shape
    w = f64(np.asarray(w, np.float32).astype(ml_dtypes.bfloat16)).reshape(k // 32, 32, n)
    amax = np.abs(w).max(1)
    if fmt == "e4m3":
        byte = np.frexp(amax)[1] - 1 + 127 - 7
    else:
        mant, ex = np.frexp(amax / 6.0)
        byte = np.where(mant > 0.5, ex, ex - 1) + 127
    byte = np.clip(np.where(amax > 0, byte, 1), 1, 254)
    scaled = (w * np.exp2(127.0 - byte)[:, None, :]).reshape(k, n).astype(np.float32)
    by_word = np.ascontiguousarray(scaled.reshape(k // 512, 128, 4, n).transpose(0, 1, 3, 2))
    if fmt == "e4m3":
        words = by_word.astype(ml_dtypes.float8_e4m3fn).view(np.uint8)
    else:
        c = by_word.astype(ml_dtypes.float4_e2m1fn).view(np.uint8) & 0xF
        words = (c[..., 0::2] | (c[..., 1::2] << 4)).reshape(k // 512, 128, 2 * n)
    return np.ascontiguousarray(words), np.ascontiguousarray(byte.astype(np.uint8).reshape(k // 512, 16, n))


def unpack_weight(words, scales, fmt):
    g, _, n = scales.shape
    words = np.ascontiguousarray(words).reshape(g, 128, n, -1)
    if fmt == "e4m3":
        vals = words.view(ml_dtypes.float8_e4m3fn).astype(np.float64)
    else:
        nib = np.empty((g, 128, n, 4), np.uint8)
        nib[..., 0::2] = words & 0xF
        nib[..., 1::2] = words >> 4
        vals = E2M1[nib]
    vals = vals * np.repeat(np.exp2(scales.astype(np.float64) - 127.0), 8, axis=1)[..., None]
    return vals.transpose(0, 1, 3, 2).reshape(g * 512, n)


K, T, J, R, N = 1024, 1024, 512, 512, 512


def setup_inputs():
    n = np.random.standard_normal
    idx = np.random.permutation(T)[:J]
    fk = mx_kscale(K)
    fr = mx_kscale(R)
    xtp = pack_weight(n((K, T)) / fk[:, None], "e4m3")
    wap = pack_weight(n((K, R)) * 1 / np.sqrt(K) * fk[:, None] * fr, "e2m1")
    wbp = pack_weight(n((R, N)) * 1 / np.sqrt(R) / fr[:, None], "e4m3")
    return {
        "xt_words": xtp[0],
        "xt_scales": xtp[1],
        "wa_words": wap[0],
        "wa_scales": wap[1],
        "old": (n((R, T)) * fr[:, None]).astype(np.float32),
        "wb_words": wbp[0],
        "wb_scales": wbp[1],
        "offs": striped(idx),
    }


def reference(xt_words, xt_scales, wa_words, wa_scales, old, wb_words, wb_scales, offs):
    idx = unstriped(offs)
    xtu = unpack_weight(xt_words, xt_scales, "e4m3")
    wau = unpack_weight(wa_words, wa_scales, "e2m1")
    wbu = unpack_weight(wb_words, wb_scales, "e4m3")
    xtidxg = xtu[:, idx]
    a = wau.T @ xtidxg
    h1 = np.maximum(a, 0.0)
    hp = np.zeros((R, T))
    hp[:, idx] = h1
    pg = hp + 0.5 * f64(old)
    pgq = mxq(pg, 0, "e4m3")
    y = wbu.T @ pgq
    return y

@@ -1,0 +1,196 @@
+from contextlib import ExitStack
+
+import concourse.mybir as mybir
+
+K, T, J, R, N = 1024, 1024, 512, 512, 512
+FLOPS = 2 * K * R * J + 2 * R * N * T
+
+F32 = mybir.dt.float32
+BF16 = mybir.dt.bfloat16
+I32 = mybir.dt.int32
+U32 = mybir.dt.uint32
+U16 = mybir.dt.uint16
+U8 = mybir.dt.uint8
+FP8X4 = mybir.dt.float8_e4m3fn_x4
+FP4X4 = mybir.dt.float4_e2m1fn_x4
+ACT = mybir.ActivationFunctionType
+ALU = mybir.AluOpType
+
+P = 128
+PACK = 4
+PASSES = K // (P * PACK)
+BANK = 512
+HALF = J // 2
+CHUNKS = (128, 256, 256, 256, 128)
+
+
+def tile_list_page_of_hidden_values_kernel(
+    tc, xt_words, xt_scales, wa_words, wa_scales, old, wb_words, wb_scales, offs, out
+):
+    nc = tc.nc
+    with ExitStack() as ctx:
+        keep = ctx.enter_context(tc.tile_pool(name="keep", bufs=1))
+        psum = ctx.enter_context(tc.psum_pool(name="psum", bufs=8))
+
+        def held(shape, dtype, name, slot=None):
+            return keep.tile(shape, dtype, name=name, tag=slot or name, align_bytes=64)
+
+        offsets = keep.tile([P, J // 16], U16, name="offsets")
+        xs = held([P, T], U8, "xs")
+        was = held([P, PASSES, R], U8, "was")
+        xw = [held([P, T], U32, "xw%d" % z) for z in range(PASSES)]
+        waw = held([P, PASSES, R], U16, "waw")
+        pages = [held([P, T], F32, "page%d" % t) for t in range(2)]
+        gs = held([P, J], U8, "gs")
+        gs1 = held([P, J], U8, "gs1")
+
+        nc.gpsimd.memset(xs[:].bitcast(I32), 0)
+        nc.gpsimd.memset(was[:].bitcast(I32), 0)
+        nc.gpsimd.memset(gs1[:].bitcast(I32), 0)
+        for t in range(2):
+            nc.vector.memset(pages[t][:], 0.0)
+
+        def load_words(tile, words):
+            nc.sync.dma_start(
+                out=tile[:].bitcast(I32), in_=words.rearrange("p c r -> p (c r)").bitcast(I32)
+            )
+
+        nc.sync.dma_start(offsets[:], offs)
+        for q in range(4):
+            nc.sync.dma_start(
+                out=xs[32 * q : 32 * q + 8].bitcast(I32),
+                in_=xt_scales[:, 4 * q : 4 * q + 4, :].bitcast(I32),
+            )
+        load_words(xw[0], xt_words[0])
+        nc.sync.dma_start(
+            out=waw[:].bitcast(I32), in_=wa_words.rearrange("z p c -> p z c").bitcast(I32)
+        )
+        load_words(xw[1], xt_words[1])
+        for q in range(4):
+            nc.sync.dma_start(
+                out=was[32 * q : 32 * q + 4].bitcast(I32),
+                in_=wa_scales[:, 4 * q : 4 * q + 4, :].rearrange("z r c -> r z c").bitcast(I32),
+            )
+
+        nc.vector.tensor_copy(gs[:], xs[:].indirect(offsets[:]))
+        for q in range(4):
+            nc.sync.dma_start(
+                out=gs1[32 * q : 32 * q + 4].bitcast(I32),
+                in_=gs[32 * q + 4 : 32 * q + 8].bitcast(I32),
+            )
+        planes = [gs, gs1]
+        gw = [held([P, J], U32, "gw%d" % z) for z in range(PASSES)]
+        wad = held([P, PASSES, PACK, P], U16, "wad")
+        wasd = held([P, PASSES, PACK, P], U8, "wasd")
+        nc.vector.tensor_copy(
+            out=wad[:].rearrange("p z t m -> p z m t"),
+            in_=waw[:].rearrange("p z (m t) -> p z m t", t=PACK),
+        )
+        for h in range(2):
+            for z in range(PASSES):
+                nc.vector.tensor_copy(
+                    gw[z][:, h * HALF : (h + 1) * HALF],
+                    xw[z][:].indirect(offsets[:, h * HALF // 16 : (h + 1) * HALF // 16]),
+                )
+            if h == 0:
+                nc.vector.tensor_copy(
+                    out=wasd[:].rearrange("p z t m -> p z m t"),
+                    in_=was[:].rearrange("p z (m t) -> p z m t", t=PACK),
+                )
+
+        old_rows = old.rearrange("(p t) c -> p t c", t=PACK)
+        olds = []
+        for t, slot in enumerate(("was", "xw0", "xw1")):
+            olds.append(held([P, T], F32, "old%d" % t, slot))
+            nc.sync.dma_start(out=olds[t][:], in_=old_rows[:, t, :])
+
+        def first_layer(t, j0, j1, width):
+            bank = psum.tile([P, BANK], F32, name="bank")
+            for c0 in range(j0, j1, width):
+                for z in range(PASSES):
+                    nc.tensor.matmul_mx(
+                        out=bank[:, c0 - j0 : c0 - j0 + width],
+                        lhsT=wad[:, z, t, :].bitcast(FP4X4),
+                        lhsT_scale=wasd[:, z, t, :],
+                        rhs=gw[z][:, c0 : c0 + width].bitcast(FP8X4),
+                        rhs_scale=planes[z][:, c0 : c0 + width],
+                        start=(z == 0),
+                        stop=(z == PASSES - 1),
+                    )
+            hidden = held([P, j1 - j0], F32, "hidden%d_%d" % (t, j0))
+            nc.scalar.activation(hidden[:], bank[:, 0 : j1 - j0], ACT.Relu)
+            nc.vector.tensor_copy(
+                pages[t][:].indirect(offsets[:, j0 // 16 : j1 // 16]), hidden[:]
+            )
+
+        first_layer(0, 0, HALF, P)
+        first_layer(0, HALF, J, P)
+        for t, slot in ((2, "hidden0_0"), (3, "hidden0_%d" % HALF)):
+            pages.append(held([P, T], F32, "page%d" % t, slot))
+            nc.gpsimd.memset(pages[t][:], 0.0)
+        for t in range(1, PACK):
+            first_layer(t, 0, J, J)
+
+        olds.append(held([P, T], F32, "old3", "gs"))
+        nc.sync.dma_start(out=olds[3][:], in_=old_rows[:, 3, :])
+        wbw = held([P, N], U32, "wbw", "gw0")
+        load_words(wbw, wb_words[0])
+        wbs = held([P, N], U8, "wbs", "gw1")
+        nc.gpsimd.memset(wbs[:].bitcast(I32), 0)
+        for q in range(4):
+            nc.sync.dma_start(
+                out=wbs[32 * q : 32 * q + 4].bitcast(I32),
+                in_=wb_scales[0, 4 * q : 4 * q + 4, :].bitcast(I32),
+            )
+
+        halves = [held([P, T], F32, "half%d" % t) for t in range(PACK - 1)]
+        for t in range(PACK - 1):
+            nc.scalar.activation(halves[t][:], olds[t][:], ACT.Copy, scale=0.5)
+
+        low = held([P, 2, T], BF16, "low")
+        for t in range(2):
+            nc.gpsimd.tensor_tensor(low[:, t, :], pages[t][:], halves[t][:], ALU.add)
+
+        starts = [sum(CHUNKS[:i]) for i in range(len(CHUNKS))]
+        woven = [held([P, w, PACK], BF16, "woven%d" % i) for i, w in enumerate(CHUNKS)]
+        high = [held([P, 2, w], BF16, "high%d" % i) for i, w in enumerate(CHUNKS)]
+        for i, w in enumerate(CHUNKS):
+            cols = slice(starts[i], starts[i] + w)
+            nc.scalar.copy(woven[i][:, :, 0:2], low[:, :, cols].rearrange("p e c -> p c e"))
+            nc.gpsimd.tensor_tensor(high[i][:, 0, :], pages[2][:, cols], halves[2][:, cols], ALU.add)
+
+        out_rows = out.rearrange("(a p) c -> p a c", p=P)
+        last = len(CHUNKS) - 1
+        for i, w in enumerate(CHUNKS):
+            cols = slice(starts[i], starts[i] + w)
+            nc.vector.scalar_tensor_tensor(
+                out=high[i][:, 1, :], in0=olds[3][:, cols], scalar=0.5, in1=pages[3][:, cols],
+                op0=ALU.mult, op1=ALU.add,
+            )
+            nc.vector.tensor_copy(woven[i][:, :, 2:4], high[i][:].rearrange("p e c -> p c e"))
+            codes = held([P, w], U32, "codes%d" % i)
+            scales = held([P, w], U8, "scales%d" % i)
+            nc.vector.quantize_mx(
+                out=codes[:].bitcast(FP8X4), scales=scales[:],
+                in_=woven[i][:].rearrange("p c t -> p (c t)"),
+            )
+            per_bank = 2
+            for a0 in range(0, N // P, per_bank):
+                bank = psum.tile([P, BANK], F32, name="bank")
+                for a in range(a0, a0 + per_bank):
+                    nc.tensor.matmul_mx(
+                        out=bank[:, (a - a0) * w : (a - a0 + 1) * w],
+                        lhsT=wbw[:, a * P : (a + 1) * P].bitcast(FP8X4),
+                        lhsT_scale=wbs[:, a * P : (a + 1) * P],
+                        rhs=codes[:].bitcast(FP8X4),
+                        rhs_scale=scales[:],
+                        start=True,
+                        stop=True,
+                    )
+                result = held([P, per_bank, w], F32, "result%d_%d" % (i, a0))
+                flat = result[:].rearrange("p a c -> p (a c)")
+                if i >= last - 1 and a0 > 0:
+                    nc.vector.tensor_copy(flat, bank[:, 0 : per_bank * w])
+                else:
+                    nc.scalar.copy(flat, bank[:, 0 : per_bank * w])
+                nc.sync.dma_start(out=out_rows[:, a0 : a0 + per_bank, cols], in_=result[:])

@@ -30,7 +30,8 @@ def tile_list_page_of_hidden_values_kernel(
     nc = tc.nc
     with ExitStack() as ctx:
         keep = ctx.enter_context(tc.tile_pool(name="keep", bufs=1))
-        psum = ctx.enter_context(tc.psum_pool(name="psum", bufs=8))
+        psum = ctx.enter_context(tc.psum_pool(name="psum", bufs=5))
+        psum_first = ctx.enter_context(tc.psum_pool(name="psum_first", bufs=3))
 
         def held(shape, dtype, name, slot=None):
             return keep.tile(shape, dtype, name=name, tag=slot or name, align_bytes=64)
@@ -38,17 +39,20 @@ def tile_list_page_of_hidden_values_kernel(
         offsets = keep.tile([P, J // 16], U16, name="offsets")
         xs = held([P, T], U8, "xs")
         was = held([P, PASSES, R], U8, "was")
-        xw = [held([P, T], U32, "xw%d" % z) for z in range(PASSES)]
+        xw = held([P, PASSES, T], U32, "xw")
         waw = held([P, PASSES, R], U16, "waw")
-        pages = [held([P, T], F32, "page%d" % t) for t in range(2)]
+        pages = [held([P, T], F32, "page%d" % t) for t in range(PACK)]
         gs = held([P, J], U8, "gs")
         gs1 = held([P, J], U8, "gs1")
 
-        nc.gpsimd.memset(xs[:].bitcast(I32), 0)
-        nc.gpsimd.memset(was[:].bitcast(I32), 0)
+        nc.gpsimd.memset(xs[:, 0 : T // 2].bitcast(I32), 0)
+        nc.vector.memset(xs[:, T // 2 : T].bitcast(I32), 0)
         nc.gpsimd.memset(gs1[:].bitcast(I32), 0)
         for t in range(2):
             nc.vector.memset(pages[t][:], 0.0)
+        nc.gpsimd.memset(pages[2][:], 0.0)
+        nc.gpsimd.memset(was[:].bitcast(I32), 0)
+        nc.gpsimd.memset(pages[3][:], 0.0)
 
         def load_words(tile, words):
             nc.sync.dma_start(
@@ -61,81 +65,88 @@ def tile_list_page_of_hidden_values_kernel(
                 out=xs[32 * q : 32 * q + 8].bitcast(I32),
                 in_=xt_scales[:, 4 * q : 4 * q + 4, :].bitcast(I32),
             )
-        load_words(xw[0], xt_words[0])
         nc.sync.dma_start(
             out=waw[:].bitcast(I32), in_=wa_words.rearrange("z p c -> p z c").bitcast(I32)
         )
-        load_words(xw[1], xt_words[1])
+        nc.sync.dma_start(
+            out=xw[:].bitcast(I32), in_=xt_words.rearrange("z p c r -> p z (c r)").bitcast(I32)
+        )
         for q in range(4):
-            nc.sync.dma_start(
+            nc.scalar.dma_start(
                 out=was[32 * q : 32 * q + 4].bitcast(I32),
                 in_=wa_scales[:, 4 * q : 4 * q + 4, :].rearrange("z r c -> r z c").bitcast(I32),
             )
 
         nc.vector.tensor_copy(gs[:], xs[:].indirect(offsets[:]))
-        for q in range(4):
-            nc.sync.dma_start(
-                out=gs1[32 * q : 32 * q + 4].bitcast(I32),
-                in_=gs[32 * q + 4 : 32 * q + 8].bitcast(I32),
+        for p0, p1 in ((0, 64), (64, 96), (96, 100)):
+            nc.scalar.dma_start(
+                out=gs1[p0:p1].bitcast(I32), in_=gs[p0 + 4 : p1 + 4].bitcast(I32)
             )
         planes = [gs, gs1]
-        gw = [held([P, J], U32, "gw%d" % z) for z in range(PASSES)]
+        gw = []
         wad = held([P, PASSES, PACK, P], U16, "wad")
         wasd = held([P, PASSES, PACK, P], U8, "wasd")
         nc.vector.tensor_copy(
             out=wad[:].rearrange("p z t m -> p z m t"),
             in_=waw[:].rearrange("p z (m t) -> p z m t", t=PACK),
         )
-        for h in range(2):
+
+        def gather_words(tile, first, j0, j1):
             for z in range(PASSES):
                 nc.vector.tensor_copy(
-                    gw[z][:, h * HALF : (h + 1) * HALF],
-                    xw[z][:].indirect(offsets[:, h * HALF // 16 : (h + 1) * HALF // 16]),
+                    tile[:, z, j0 - first : j1 - first],
+                    xw[:, z, :].indirect(offsets[:, j0 // 16 : j1 // 16]),
                 )
-            if h == 0:
-                nc.vector.tensor_copy(
-                    out=wasd[:].rearrange("p z t m -> p z m t"),
-                    in_=was[:].rearrange("p z (m t) -> p z m t", t=PACK),
-                )
+
+        gw.append(held([P, PASSES, P], U32, "gw0"))
+        gather_words(gw[0], 0, 0, P)
+        nc.vector.tensor_copy(
+            out=wasd[:].rearrange("p z t m -> p z m t"),
+            in_=was[:].rearrange("p z (m t) -> p z m t", t=PACK),
+        )
+        gw.append(held([P, PASSES, J - P], U32, "gw1", "was"))
+        gather_words(gw[1], P, P, HALF)
+        gather_words(gw[1], P, HALF, J)
 
         old_rows = old.rearrange("(p t) c -> p t c", t=PACK)
         olds = []
-        for t, slot in enumerate(("was", "xw0", "xw1")):
+        for t, slot in enumerate(("waw", "xw")):
             olds.append(held([P, T], F32, "old%d" % t, slot))
             nc.sync.dma_start(out=olds[t][:], in_=old_rows[:, t, :])
 
-        def first_layer(t, j0, j1, width):
-            bank = psum.tile([P, BANK], F32, name="bank")
+        def first_layer(t, j0, j1):
+            width = P
+            bank = psum_first.tile([P, BANK], F32, name="bank")
             for c0 in range(j0, j1, width):
                 for z in range(PASSES):
                     nc.tensor.matmul_mx(
                         out=bank[:, c0 - j0 : c0 - j0 + width],
                         lhsT=wad[:, z, t, :].bitcast(FP4X4),
                         lhsT_scale=wasd[:, z, t, :],
-                        rhs=gw[z][:, c0 : c0 + width].bitcast(FP8X4),
+                        rhs=(gw[0][:, z, :] if c0 == 0 else gw[1][:, z, c0 - P : c0]).bitcast(FP8X4),
                         rhs_scale=planes[z][:, c0 : c0 + width],
                         start=(z == 0),
                         stop=(z == PASSES - 1),
                     )
             hidden = held([P, j1 - j0], F32, "hidden%d_%d" % (t, j0))
-            nc.scalar.activation(hidden[:], bank[:, 0 : j1 - j0], ACT.Relu)
+            nc.scalar.activation(hidden[:], bank[:, 0 : j1 - j0], ACT.Relu, scale=2.0)
             nc.vector.tensor_copy(
                 pages[t][:].indirect(offsets[:, j0 // 16 : j1 // 16]), hidden[:]
             )
 
-        first_layer(0, 0, HALF, P)
-        first_layer(0, HALF, J, P)
-        for t, slot in ((2, "hidden0_0"), (3, "hidden0_%d" % HALF)):
-            pages.append(held([P, T], F32, "page%d" % t, slot))
-            nc.gpsimd.memset(pages[t][:], 0.0)
-        for t in range(1, PACK):
-            first_layer(t, 0, J, J)
+        first_layer(0, 0, P)
+        first_layer(1, 0, P)
+        first_layer(0, P, HALF)
+        first_layer(0, HALF, J)
+        first_layer(1, P, J)
+        for t in range(2, PACK):
+            first_layer(t, 0, J)
 
-        olds.append(held([P, T], F32, "old3", "gs"))
-        nc.sync.dma_start(out=olds[3][:], in_=old_rows[:, 3, :])
+        olds.append(held([P, T], F32, "old2", "hidden0_0"))
+        nc.sync.dma_start(out=olds[2][:], in_=old_rows[:, 2, :])
         wbw = held([P, N], U32, "wbw", "gw0")
         load_words(wbw, wb_words[0])
-        wbs = held([P, N], U8, "wbs", "gw1")
+        wbs = held([P, N], U8, "wbs", "xs")
         nc.gpsimd.memset(wbs[:].bitcast(I32), 0)
         for q in range(4):
             nc.sync.dma_start(
@@ -143,31 +154,30 @@ def tile_list_page_of_hidden_values_kernel(
                 in_=wb_scales[0, 4 * q : 4 * q + 4, :].bitcast(I32),
             )
 
-        halves = [held([P, T], F32, "half%d" % t) for t in range(PACK - 1)]
-        for t in range(PACK - 1):
-            nc.scalar.activation(halves[t][:], olds[t][:], ACT.Copy, scale=0.5)
-
         low = held([P, 2, T], BF16, "low")
         for t in range(2):
-            nc.gpsimd.tensor_tensor(low[:, t, :], pages[t][:], halves[t][:], ALU.add)
+            nc.gpsimd.tensor_tensor(low[:, t, :], pages[t][:], olds[t][:], ALU.add)
+        olds.append(held([P, T], F32, "old3", "page1"))
+        nc.sync.dma_start(out=olds[3][:], in_=old_rows[:, 3, :])
+        high = held([P, 2, T], BF16, "high")
+        nc.gpsimd.tensor_tensor(high[:, 0, :], pages[2][:], olds[2][:], ALU.add)
 
         starts = [sum(CHUNKS[:i]) for i in range(len(CHUNKS))]
         woven = [held([P, w, PACK], BF16, "woven%d" % i) for i, w in enumerate(CHUNKS)]
-        high = [held([P, 2, w], BF16, "high%d" % i) for i, w in enumerate(CHUNKS)]
         for i, w in enumerate(CHUNKS):
             cols = slice(starts[i], starts[i] + w)
-            nc.scalar.copy(woven[i][:, :, 0:2], low[:, :, cols].rearrange("p e c -> p c e"))
-            nc.gpsimd.tensor_tensor(high[i][:, 0, :], pages[2][:, cols], halves[2][:, cols], ALU.add)
+            nc.scalar.activation(
+                woven[i][:, :, 0:2], low[:, :, cols].rearrange("p e c -> p c e"), ACT.Copy, scale=0.5
+            )
 
         out_rows = out.rearrange("(a p) c -> p a c", p=P)
         last = len(CHUNKS) - 1
         for i, w in enumerate(CHUNKS):
             cols = slice(starts[i], starts[i] + w)
-            nc.vector.scalar_tensor_tensor(
-                out=high[i][:, 1, :], in0=olds[3][:, cols], scalar=0.5, in1=pages[3][:, cols],
-                op0=ALU.mult, op1=ALU.add,
+            nc.vector.tensor_tensor(high[:, 1, cols], pages[3][:, cols], olds[3][:, cols], ALU.add)
+            nc.vector.tensor_scalar_mul(
+                woven[i][:, :, 2:4], high[:, :, cols].rearrange("p e c -> p c e"), 0.5
             )
-            nc.vector.tensor_copy(woven[i][:, :, 2:4], high[i][:].rearrange("p e c -> p c e"))
             codes = held([P, w], U32, "codes%d" % i)
             scales = held([P, w], U8, "scales%d" % i)
             nc.vector.quantize_mx(

@@ -1,6 +1,7 @@
 from contextlib import ExitStack
 
 import concourse.mybir as mybir
+from concourse.masks import make_identity
 
 K, T, J, R, N = 1024, 1024, 512, 512, 512
 FLOPS = 2 * K * R * J + 2 * R * N * T
@@ -31,7 +32,7 @@ def tile_list_page_of_hidden_values_kernel(
     with ExitStack() as ctx:
         keep = ctx.enter_context(tc.tile_pool(name="keep", bufs=1))
         psum = ctx.enter_context(tc.psum_pool(name="psum", bufs=5))
-        psum_first = ctx.enter_context(tc.psum_pool(name="psum_first", bufs=3))
+        psum_turn = ctx.enter_context(tc.psum_pool(name="psum_turn", bufs=3))
 
         def held(shape, dtype, name, slot=None):
             return keep.tile(shape, dtype, name=name, tag=slot or name, align_bytes=64)
@@ -48,11 +49,14 @@ def tile_list_page_of_hidden_values_kernel(
         nc.gpsimd.memset(xs[:, 0 : T // 2].bitcast(I32), 0)
         nc.vector.memset(xs[:, T // 2 : T].bitcast(I32), 0)
         nc.gpsimd.memset(gs1[:].bitcast(I32), 0)
-        for t in range(2):
+        for t in range(PACK - 1):
             nc.vector.memset(pages[t][:], 0.0)
-        nc.gpsimd.memset(pages[2][:], 0.0)
+        ident32 = held([P, P], F32, "ident32")
+        ident16 = held([P, P], BF16, "ident16")
+        make_identity(nc, ident32[:])
         nc.gpsimd.memset(was[:].bitcast(I32), 0)
-        nc.gpsimd.memset(pages[3][:], 0.0)
+        nc.gpsimd.memset(pages[PACK - 1][:], 0.0)
+        make_identity(nc, ident16[:])
 
         def load_words(tile, words):
             nc.sync.dma_start(
@@ -116,7 +120,7 @@ def tile_list_page_of_hidden_values_kernel(
 
         def first_layer(t, j0, j1):
             width = P
-            bank = psum_first.tile([P, BANK], F32, name="bank")
+            bank = psum.tile([P, BANK], F32, name="bank")
             for c0 in range(j0, j1, width):
                 for z in range(PASSES):
                     nc.tensor.matmul_mx(
@@ -129,7 +133,7 @@ def tile_list_page_of_hidden_values_kernel(
                         stop=(z == PASSES - 1),
                     )
             hidden = held([P, j1 - j0], F32, "hidden%d_%d" % (t, j0))
-            nc.scalar.activation(hidden[:], bank[:, 0 : j1 - j0], ACT.Relu, scale=2.0)
+            nc.scalar.activation(hidden[:], bank[:, 0 : j1 - j0], ACT.Relu, scale=2.0 if t < PACK - 1 else 1.0)
             nc.vector.tensor_copy(
                 pages[t][:].indirect(offsets[:, j0 // 16 : j1 // 16]), hidden[:]
             )
@@ -146,7 +150,7 @@ def tile_list_page_of_hidden_values_kernel(
         nc.sync.dma_start(out=olds[2][:], in_=old_rows[:, 2, :])
         wbw = held([P, N], U32, "wbw", "gw0")
         load_words(wbw, wb_words[0])
-        wbs = held([P, N], U8, "wbs", "xs")
+        wbs = held([P, N], U8, "wbs", "wasd")
         nc.gpsimd.memset(wbs[:].bitcast(I32), 0)
         for q in range(4):
             nc.sync.dma_start(
@@ -154,30 +158,80 @@ def tile_list_page_of_hidden_values_kernel(
                 in_=wb_scales[0, 4 * q : 4 * q + 4, :].bitcast(I32),
             )
 
-        low = held([P, 2, T], BF16, "low")
-        for t in range(2):
-            nc.gpsimd.tensor_tensor(low[:, t, :], pages[t][:], olds[t][:], ALU.add)
-        olds.append(held([P, T], F32, "old3", "page1"))
-        nc.sync.dma_start(out=olds[3][:], in_=old_rows[:, 3, :])
-        high = held([P, 2, T], BF16, "high")
-        nc.gpsimd.tensor_tensor(high[:, 0, :], pages[2][:], olds[2][:], ALU.add)
+        def turn(dst, src, start, stop):
+            nc.tensor.matmul(dst, src, ident32[:], start=start, stop=stop, is_transpose=True)
+
+        sums = [psum.tile([P, 2, 2, P], F32, name="bank") for k in range(4)]
+        sources = (olds[0], olds[1], pages[0], pages[1])
+        for s, src in enumerate(sources):
+            for b in range(T // P):
+                turn(
+                    sums[b // 2][:, s % 2, b % 2, :], src[:, b * P : (b + 1) * P],
+                    s == 0 and b % 2 == 0, s == 3 and b % 2 == 1,
+                )
+        pairs = [held([P, 2, P, 2], BF16, "pairs%d" % k) for k in range(4)]
+        for k in range(4):
+            nc.scalar.activation(
+                pairs[k][:], sums[k][:].rearrange("q e b p -> q b p e"), ACT.Copy, scale=0.5
+            )
 
         starts = [sum(CHUNKS[:i]) for i in range(len(CHUNKS))]
         woven = [held([P, w, PACK], BF16, "woven%d" % i) for i, w in enumerate(CHUNKS)]
-        for i, w in enumerate(CHUNKS):
-            cols = slice(starts[i], starts[i] + w)
-            nc.scalar.activation(
-                woven[i][:, :, 0:2], low[:, :, cols].rearrange("p e c -> p c e"), ACT.Copy, scale=0.5
-            )
+        high = held([P, 2, T], BF16, "high")
+
+        def weave_low(i):
+            w = CHUNKS[i]
+            words = psum_turn.tile([P, BANK], F32, name="turned")
+            for b in range(starts[i] // P, (starts[i] + w) // P):
+                nc.tensor.transpose(
+                    words[:, b * P - starts[i] : (b + 1) * P - starts[i]],
+                    pairs[b // 2][:, b % 2].rearrange("q p e -> q (p e)").bitcast(F32),
+                    ident32[:],
+                )
+            as_words = woven[i][:].rearrange("p c t -> p (c t)").bitcast(F32)
+            nc.scalar.copy(as_words.rearrange("p (c u) -> p c u", u=2)[:, :, 0], words[:, 0:w])
+
+        def sum_plane2(b0, b1):
+            bank = psum_turn.tile([P, b1 - b0, P], F32, name="turned")
+            for s, src in enumerate((olds[2], pages[2])):
+                for b in range(b0, b1):
+                    turn(
+                        bank[:, b - b0, :], src[:, b * P : (b + 1) * P],
+                        s == 0 and b == b0, s == 1 and b == b1 - 1,
+                    )
+            rounded = held([P, b1 - b0, P], BF16, "rounded%d" % b0)
+            nc.scalar.activation(rounded[:], bank[:], ACT.Copy, scale=0.5)
+            return rounded
+
+        def return_plane2(b0, b1, rounded):
+            bank = psum_turn.tile([P, b1 - b0, P], BF16, name="turned")
+            for b in range(b1 - b0):
+                nc.tensor.transpose(bank[:, b, :], rounded[:, b, :], ident16[:])
+            nc.scalar.copy(high[:, 0, b0 * P : b1 * P], bank[:].rearrange("p b c -> p (b c)"))
+
+        for i in range(3):
+            weave_low(i)
+        first = sum_plane2(0, 2)
+        second = sum_plane2(2, 5)
+        return_plane2(0, 2, first)
+        third = sum_plane2(5, 8)
+        return_plane2(2, 5, second)
+        weave_low(3)
+        return_plane2(5, 8, third)
+        weave_low(4)
+
+        olds.append(held([P, T], F32, "old3", "pairs1"))
+        nc.sync.dma_start(out=olds[3][:], in_=old_rows[:, 3, :])
 
         out_rows = out.rearrange("(a p) c -> p a c", p=P)
         last = len(CHUNKS) - 1
         for i, w in enumerate(CHUNKS):
             cols = slice(starts[i], starts[i] + w)
-            nc.vector.tensor_tensor(high[:, 1, cols], pages[3][:, cols], olds[3][:, cols], ALU.add)
-            nc.vector.tensor_scalar_mul(
-                woven[i][:, :, 2:4], high[:, :, cols].rearrange("p e c -> p c e"), 0.5
+            nc.vector.scalar_tensor_tensor(
+                out=high[:, 1, cols], in0=olds[3][:, cols], scalar=0.5, in1=pages[3][:, cols],
+                op0=ALU.mult, op1=ALU.add,
             )
+            nc.vector.tensor_copy(woven[i][:, :, 2:4], high[:, :, cols].rearrange("p e c -> p c e"))
             codes = held([P, w], U32, "codes%d" % i)
             scales = held([P, w], U8, "scales%d" % i)
             nc.vector.quantize_mx(

@@ -22,7 +22,7 @@ PACK = 4
 PASSES = K // (P * PACK)
 BANK = 512
 HALF = J // 2
-CHUNKS = (128, 256, 256, 256, 128)
+CHUNKS = (128, 128, 256, 512)
 
 
 def tile_list_page_of_hidden_values_kernel(
@@ -31,8 +31,8 @@ def tile_list_page_of_hidden_values_kernel(
     nc = tc.nc
     with ExitStack() as ctx:
         keep = ctx.enter_context(tc.tile_pool(name="keep", bufs=1))
-        psum = ctx.enter_context(tc.psum_pool(name="psum", bufs=5))
-        psum_turn = ctx.enter_context(tc.psum_pool(name="psum_turn", bufs=3))
+        psum = ctx.enter_context(tc.psum_pool(name="psum", bufs=4))
+        psum_turn = ctx.enter_context(tc.psum_pool(name="psum_turn", bufs=4))
 
         def held(shape, dtype, name, slot=None):
             return keep.tile(shape, dtype, name=name, tag=slot or name, align_bytes=64)
@@ -42,7 +42,7 @@ def tile_list_page_of_hidden_values_kernel(
         was = held([P, PASSES, R], U8, "was")
         xw = held([P, PASSES, T], U32, "xw")
         waw = held([P, PASSES, R], U16, "waw")
-        pages = [held([P, T], F32, "page%d" % t) for t in range(PACK)]
+        pages = [held([P, T], F32, "page%d" % t) for t in range(PACK - 1)]
         gs = held([P, J], U8, "gs")
         gs1 = held([P, J], U8, "gs1")
 
@@ -55,8 +55,6 @@ def tile_list_page_of_hidden_values_kernel(
         ident16 = held([P, P], BF16, "ident16")
         make_identity(nc, ident32[:])
         nc.gpsimd.memset(was[:].bitcast(I32), 0)
-        nc.gpsimd.memset(pages[PACK - 1][:], 0.0)
-        make_identity(nc, ident16[:])
 
         def load_words(tile, words):
             nc.sync.dma_start(
@@ -112,11 +110,14 @@ def tile_list_page_of_hidden_values_kernel(
         gather_words(gw[1], P, P, HALF)
         gather_words(gw[1], P, HALF, J)
 
+        pages.append(held([P, T], F32, "page3", "waw"))
+        nc.vector.memset(pages[3][:], 0.0)
+        nc.vector.tensor_copy(ident16[:], ident32[:])
+
         old_rows = old.rearrange("(p t) c -> p t c", t=PACK)
-        olds = []
-        for t, slot in enumerate(("waw", "xw")):
-            olds.append(held([P, T], F32, "old%d" % t, slot))
-            nc.sync.dma_start(out=olds[t][:], in_=old_rows[:, t, :])
+        old_low = held([P, 2, T], F32, "old_low", "xw")
+        nc.sync.dma_start(out=old_low[:], in_=old_rows[:, 0:2, :])
+        olds = [old_low[:, 0, :], old_low[:, 1, :]]
 
         def first_layer(t, j0, j1):
             width = P
@@ -133,7 +134,7 @@ def tile_list_page_of_hidden_values_kernel(
                         stop=(z == PASSES - 1),
                     )
             hidden = held([P, j1 - j0], F32, "hidden%d_%d" % (t, j0))
-            nc.scalar.activation(hidden[:], bank[:, 0 : j1 - j0], ACT.Relu, scale=2.0 if t < PACK - 1 else 1.0)
+            nc.scalar.activation(hidden[:], bank[:, 0 : j1 - j0], ACT.Relu, scale=2.0)
             nc.vector.tensor_copy(
                 pages[t][:].indirect(offsets[:, j0 // 16 : j1 // 16]), hidden[:]
             )
@@ -189,7 +190,10 @@ def tile_list_page_of_hidden_values_kernel(
                     ident32[:],
                 )
             as_words = woven[i][:].rearrange("p c t -> p (c t)").bitcast(F32)
-            nc.scalar.copy(as_words.rearrange("p (c u) -> p c u", u=2)[:, :, 0], words[:, 0:w])
+            nc.scalar.copy(
+                as_words.rearrange("p (c u) -> p c u", u=2),
+                words[:, 0:w].rearrange("p (c o) -> p c o", o=1).to_broadcast([P, w, 2]),
+            )
 
         def sum_plane2(b0, b1):
             bank = psum_turn.tile([P, b1 - b0, P], F32, name="turned")
@@ -200,7 +204,7 @@ def tile_list_page_of_hidden_values_kernel(
                         s == 0 and b == b0, s == 1 and b == b1 - 1,
                     )
             rounded = held([P, b1 - b0, P], BF16, "rounded%d" % b0)
-            nc.scalar.activation(rounded[:], bank[:], ACT.Copy, scale=0.5)
+            nc.scalar.copy(rounded[:], bank[:])
             return rounded
 
         def return_plane2(b0, b1, rounded):
@@ -209,16 +213,12 @@ def tile_list_page_of_hidden_values_kernel(
                 nc.tensor.transpose(bank[:, b, :], rounded[:, b, :], ident16[:])
             nc.scalar.copy(high[:, 0, b0 * P : b1 * P], bank[:].rearrange("p b c -> p (b c)"))
 
-        for i in range(3):
+        for i in range(len(CHUNKS)):
             weave_low(i)
-        first = sum_plane2(0, 2)
-        second = sum_plane2(2, 5)
-        return_plane2(0, 2, first)
-        third = sum_plane2(5, 8)
-        return_plane2(2, 5, second)
-        weave_low(3)
-        return_plane2(5, 8, third)
-        weave_low(4)
+        pieces = ((2, 4), (4, 8))
+        rounded = [sum_plane2(b0, b1) for b0, b1 in pieces]
+        for (b0, b1), tile in zip(pieces, rounded):
+            return_plane2(b0, b1, tile)
 
         olds.append(held([P, T], F32, "old3", "pairs1"))
         nc.sync.dma_start(out=olds[3][:], in_=old_rows[:, 3, :])
@@ -227,18 +227,20 @@ def tile_list_page_of_hidden_values_kernel(
         last = len(CHUNKS) - 1
         for i, w in enumerate(CHUNKS):
             cols = slice(starts[i], starts[i] + w)
-            nc.vector.scalar_tensor_tensor(
-                out=high[:, 1, cols], in0=olds[3][:, cols], scalar=0.5, in1=pages[3][:, cols],
-                op0=ALU.mult, op1=ALU.add,
+            for t in range(2 if starts[i] < pieces[0][0] * P else 3, PACK):
+                nc.vector.tensor_tensor(
+                    high[:, t - 2, cols], pages[t][:, cols], olds[t][:, cols], ALU.add
+                )
+            nc.vector.tensor_scalar_mul(
+                woven[i][:, :, 2:4], high[:, :, cols].rearrange("p e c -> p c e"), 0.5
             )
-            nc.vector.tensor_copy(woven[i][:, :, 2:4], high[:, :, cols].rearrange("p e c -> p c e"))
             codes = held([P, w], U32, "codes%d" % i)
             scales = held([P, w], U8, "scales%d" % i)
             nc.vector.quantize_mx(
                 out=codes[:].bitcast(FP8X4), scales=scales[:],
                 in_=woven[i][:].rearrange("p c t -> p (c t)"),
             )
-            per_bank = 2
+            per_bank = min(2, BANK // w)
             for a0 in range(0, N // P, per_bank):
                 bank = psum.tile([P, BANK], F32, name="bank")
                 for a in range(a0, a0 + per_bank):
@@ -253,7 +255,7 @@ def tile_list_page_of_hidden_values_kernel(
                     )
                 result = held([P, per_bank, w], F32, "result%d_%d" % (i, a0))
                 flat = result[:].rearrange("p a c -> p (a c)")
-                if i >= last - 1 and a0 > 0:
+                if i == last and a0 % 2 == 1:
                     nc.vector.tensor_copy(flat, bank[:, 0 : per_bank * w])
                 else:
                     nc.scalar.copy(flat, bank[:, 0 : per_bank * w])

from contextlib import ExitStack

import concourse.mybir as mybir
from concourse.masks import make_identity

K, T, J, R, N = 1024, 1024, 512, 512, 512
FLOPS = 2 * K * R * J + 2 * R * N * T

F32 = mybir.dt.float32
BF16 = mybir.dt.bfloat16
I32 = mybir.dt.int32
U32 = mybir.dt.uint32
U16 = mybir.dt.uint16
U8 = mybir.dt.uint8
FP8X4 = mybir.dt.float8_e4m3fn_x4
FP4X4 = mybir.dt.float4_e2m1fn_x4
ACT = mybir.ActivationFunctionType
ALU = mybir.AluOpType

P = 128
PACK = 4
PASSES = K // (P * PACK)
BANK = 512
HALF = J // 2
CHUNKS = (128, 128, 256, 512)


def tile_list_page_of_hidden_values_kernel(
    tc, xt_words, xt_scales, wa_words, wa_scales, old, wb_words, wb_scales, offs, out
):
    nc = tc.nc
    with ExitStack() as ctx:
        keep = ctx.enter_context(tc.tile_pool(name="keep", bufs=1))
        psum = ctx.enter_context(tc.psum_pool(name="psum", bufs=4))
        psum_turn = ctx.enter_context(tc.psum_pool(name="psum_turn", bufs=4))

        def held(shape, dtype, name, slot=None):
            return keep.tile(shape, dtype, name=name, tag=slot or name, align_bytes=64)

        offsets = keep.tile([P, J // 16], U16, name="offsets")
        xs = held([P, T], U8, "xs")
        was = held([P, PASSES, R], U8, "was")
        xw = held([P, PASSES, T], U32, "xw")
        waw = held([P, PASSES, R], U16, "waw")
        pages = [held([P, T], F32, "page%d" % t) for t in range(PACK - 1)]
        gs = held([P, J], U8, "gs")
        gs1 = held([P, J], U8, "gs1")

        nc.gpsimd.memset(xs[:, 0 : T // 2].bitcast(I32), 0)
        nc.vector.memset(xs[:, T // 2 : T].bitcast(I32), 0)
        nc.gpsimd.memset(gs1[:].bitcast(I32), 0)
        for t in range(PACK - 1):
            nc.vector.memset(pages[t][:], 0.0)
        ident32 = held([P, P], F32, "ident32")
        ident16 = held([P, P], BF16, "ident16")
        make_identity(nc, ident32[:])
        nc.gpsimd.memset(was[:].bitcast(I32), 0)

        def load_words(tile, words):
            nc.sync.dma_start(
                out=tile[:].bitcast(I32), in_=words.rearrange("p c r -> p (c r)").bitcast(I32)
            )

        nc.sync.dma_start(offsets[:], offs)
        for q in range(4):
            nc.sync.dma_start(
                out=xs[32 * q : 32 * q + 8].bitcast(I32),
                in_=xt_scales[:, 4 * q : 4 * q + 4, :].bitcast(I32),
            )
        nc.sync.dma_start(
            out=waw[:].bitcast(I32), in_=wa_words.rearrange("z p c -> p z c").bitcast(I32)
        )
        nc.sync.dma_start(
            out=xw[:].bitcast(I32), in_=xt_words.rearrange("z p c r -> p z (c r)").bitcast(I32)
        )
        for q in range(4):
            nc.scalar.dma_start(
                out=was[32 * q : 32 * q + 4].bitcast(I32),
                in_=wa_scales[:, 4 * q : 4 * q + 4, :].rearrange("z r c -> r z c").bitcast(I32),
            )

        nc.vector.tensor_copy(gs[:], xs[:].indirect(offsets[:]))
        for p0, p1 in ((0, 64), (64, 96), (96, 100)):
            nc.scalar.dma_start(
                out=gs1[p0:p1].bitcast(I32), in_=gs[p0 + 4 : p1 + 4].bitcast(I32)
            )
        planes = [gs, gs1]
        gw = []
        wad = held([P, PASSES, PACK, P], U16, "wad")
        wasd = held([P, PASSES, PACK, P], U8, "wasd")
        nc.vector.tensor_copy(
            out=wad[:].rearrange("p z t m -> p z m t"),
            in_=waw[:].rearrange("p z (m t) -> p z m t", t=PACK),
        )

        def gather_words(tile, first, j0, j1):
            for z in range(PASSES):
                nc.vector.tensor_copy(
                    tile[:, z, j0 - first : j1 - first],
                    xw[:, z, :].indirect(offsets[:, j0 // 16 : j1 // 16]),
                )

        gw.append(held([P, PASSES, P], U32, "gw0"))
        gather_words(gw[0], 0, 0, P)
        nc.vector.tensor_copy(
            out=wasd[:].rearrange("p z t m -> p z m t"),
            in_=was[:].rearrange("p z (m t) -> p z m t", t=PACK),
        )
        gw.append(held([P, PASSES, J - P], U32, "gw1", "was"))
        gather_words(gw[1], P, P, HALF)
        gather_words(gw[1], P, HALF, J)

        pages.append(held([P, T], F32, "page3", "waw"))
        nc.vector.memset(pages[3][:], 0.0)
        nc.vector.tensor_copy(ident16[:], ident32[:])

        old_rows = old.rearrange("(p t) c -> p t c", t=PACK)
        old_low = held([P, 2, T], F32, "old_low", "xw")
        nc.sync.dma_start(out=old_low[:], in_=old_rows[:, 0:2, :])
        olds = [old_low[:, 0, :], old_low[:, 1, :]]

        def first_layer(t, j0, j1):
            width = P
            bank = psum.tile([P, BANK], F32, name="bank")
            for c0 in range(j0, j1, width):
                for z in range(PASSES):
                    nc.tensor.matmul_mx(
                        out=bank[:, c0 - j0 : c0 - j0 + width],
                        lhsT=wad[:, z, t, :].bitcast(FP4X4),
                        lhsT_scale=wasd[:, z, t, :],
                        rhs=(gw[0][:, z, :] if c0 == 0 else gw[1][:, z, c0 - P : c0]).bitcast(FP8X4),
                        rhs_scale=planes[z][:, c0 : c0 + width],
                        start=(z == 0),
                        stop=(z == PASSES - 1),
                    )
            hidden = held([P, j1 - j0], F32, "hidden%d_%d" % (t, j0))
            nc.scalar.activation(hidden[:], bank[:, 0 : j1 - j0], ACT.Relu, scale=2.0)
            nc.vector.tensor_copy(
                pages[t][:].indirect(offsets[:, j0 // 16 : j1 // 16]), hidden[:]
            )

        first_layer(0, 0, P)
        first_layer(1, 0, P)
        first_layer(0, P, HALF)
        first_layer(0, HALF, J)
        first_layer(1, P, J)
        for t in range(2, PACK):
            first_layer(t, 0, J)

        olds.append(held([P, T], F32, "old2", "hidden0_0"))
        nc.sync.dma_start(out=olds[2][:], in_=old_rows[:, 2, :])
        wbw = held([P, N], U32, "wbw", "gw0")
        load_words(wbw, wb_words[0])
        wbs = held([P, N], U8, "wbs", "wasd")
        nc.gpsimd.memset(wbs[:].bitcast(I32), 0)
        for q in range(4):
            nc.sync.dma_start(
                out=wbs[32 * q : 32 * q + 4].bitcast(I32),
                in_=wb_scales[0, 4 * q : 4 * q + 4, :].bitcast(I32),
            )

        def turn(dst, src, start, stop):
            nc.tensor.matmul(dst, src, ident32[:], start=start, stop=stop, is_transpose=True)

        sums = [psum.tile([P, 2, 2, P], F32, name="bank") for k in range(4)]
        sources = (olds[0], olds[1], pages[0], pages[1])
        for s, src in enumerate(sources):
            for b in range(T // P):
                turn(
                    sums[b // 2][:, s % 2, b % 2, :], src[:, b * P : (b + 1) * P],
                    s == 0 and b % 2 == 0, s == 3 and b % 2 == 1,
                )
        pairs = [held([P, 2, P, 2], BF16, "pairs%d" % k) for k in range(4)]
        for k in range(4):
            nc.scalar.activation(
                pairs[k][:], sums[k][:].rearrange("q e b p -> q b p e"), ACT.Copy, scale=0.5
            )

        starts = [sum(CHUNKS[:i]) for i in range(len(CHUNKS))]
        woven = [held([P, w, PACK], BF16, "woven%d" % i) for i, w in enumerate(CHUNKS)]
        high = held([P, 2, T], BF16, "high")

        def weave_low(i):
            w = CHUNKS[i]
            words = psum_turn.tile([P, BANK], F32, name="turned")
            for b in range(starts[i] // P, (starts[i] + w) // P):
                nc.tensor.transpose(
                    words[:, b * P - starts[i] : (b + 1) * P - starts[i]],
                    pairs[b // 2][:, b % 2].rearrange("q p e -> q (p e)").bitcast(F32),
                    ident32[:],
                )
            as_words = woven[i][:].rearrange("p c t -> p (c t)").bitcast(F32)
            nc.scalar.copy(
                as_words.rearrange("p (c u) -> p c u", u=2),
                words[:, 0:w].rearrange("p (c o) -> p c o", o=1).to_broadcast([P, w, 2]),
            )

        def sum_plane2(b0, b1):
            bank = psum_turn.tile([P, b1 - b0, P], F32, name="turned")
            for s, src in enumerate((olds[2], pages[2])):
                for b in range(b0, b1):
                    turn(
                        bank[:, b - b0, :], src[:, b * P : (b + 1) * P],
                        s == 0 and b == b0, s == 1 and b == b1 - 1,
                    )
            rounded = held([P, b1 - b0, P], BF16, "rounded%d" % b0)
            nc.scalar.copy(rounded[:], bank[:])
            return rounded

        def return_plane2(b0, b1, rounded):
            bank = psum_turn.tile([P, b1 - b0, P], BF16, name="turned")
            for b in range(b1 - b0):
                nc.tensor.transpose(bank[:, b, :], rounded[:, b, :], ident16[:])
            nc.scalar.copy(high[:, 0, b0 * P : b1 * P], bank[:].rearrange("p b c -> p (b c)"))

        for i in range(len(CHUNKS)):
            weave_low(i)
        pieces = ((2, 4), (4, 8))
        rounded = [sum_plane2(b0, b1) for b0, b1 in pieces]
        for (b0, b1), tile in zip(pieces, rounded):
            return_plane2(b0, b1, tile)

        olds.append(held([P, T], F32, "old3", "pairs1"))
        nc.sync.dma_start(out=olds[3][:], in_=old_rows[:, 3, :])

        out_rows = out.rearrange("(a p) c -> p a c", p=P)
        last = len(CHUNKS) - 1
        for i, w in enumerate(CHUNKS):
            cols = slice(starts[i], starts[i] + w)
            for t in range(2 if starts[i] < pieces[0][0] * P else 3, PACK):
                nc.vector.tensor_tensor(
                    high[:, t - 2, cols], pages[t][:, cols], olds[t][:, cols], ALU.add
                )
            nc.vector.tensor_scalar_mul(
                woven[i][:, :, 2:4], high[:, :, cols].rearrange("p e c -> p c e"), 0.5
            )
            codes = held([P, w], U32, "codes%d" % i)
            scales = held([P, w], U8, "scales%d" % i)
            nc.vector.quantize_mx(
                out=codes[:].bitcast(FP8X4), scales=scales[:],
                in_=woven[i][:].rearrange("p c t -> p (c t)"),
            )
            per_bank = min(2, BANK // w)
            for a0 in range(0, N // P, per_bank):
                bank = psum.tile([P, BANK], F32, name="bank")
                for a in range(a0, a0 + per_bank):
                    nc.tensor.matmul_mx(
                        out=bank[:, (a - a0) * w : (a - a0 + 1) * w],
                        lhsT=wbw[:, a * P : (a + 1) * P].bitcast(FP8X4),
                        lhsT_scale=wbs[:, a * P : (a + 1) * P],
                        rhs=codes[:].bitcast(FP8X4),
                        rhs_scale=scales[:],
                        start=True,
                        stop=True,
                    )
                result = held([P, per_bank, w], F32, "result%d_%d" % (i, a0))
                flat = result[:].rearrange("p a c -> p (a c)")
                if i == last and a0 % 2 == 1:
                    nc.vector.tensor_copy(flat, bank[:, 0 : per_bank * w])
                else:
                    nc.scalar.copy(flat, bank[:, 0 : per_bank * w])
                nc.sync.dma_start(out=out_rows[:, a0 : a0 + per_bank, cols], in_=result[:])
